import numpy as np, ml_dtypes
CORES = [66,74,82,90,194,202,210,218]
N = 8
import mx_ref
BF = ml_dtypes.bfloat16
def cols(t, e):
    v = np.concatenate([t.reshape(128, -1, 4), np.zeros((128, 1, 4), BF)], axis=1)
    return np.ascontiguousarray(v[:, e]).reshape(128, -1)
def pick(q, e):
    c = np.concatenate([q[0].reshape(128, -1, 4), np.zeros((128, 1, 4), np.uint8)], axis=1); s = np.concatenate([q[1], np.ones((16, 1), np.uint8)], axis=1)
    return (np.ascontiguousarray(c[:, e].reshape(128, -1)), np.ascontiguousarray(s[:, e]))
def join(*qs):
    return (np.concatenate([q[0] for q in qs], axis=1), np.concatenate([q[1] for q in qs], axis=1))
def put(q, e, v):
    c, s = q[0].reshape(128, -1, 4).copy(), q[1].copy(); c[:, e] = v[0].reshape(128, -1, 4); s[:, e] = v[1]
    return (c.reshape(128, -1), s)
def pk(c, s):
    return (np.ascontiguousarray(c), mx_ref.live(s))
def emit(q):
    return q[0], q[1]
def decode(q):
    o = []
    for b in range(4):
        e = np.zeros((128, 128, 4), np.float32); e[np.arange(128), np.arange(128), b] = 1
        o.append(mx_ref.matmul(mx_ref.quantize(e.reshape(128, 512).astype(BF)), q))
    return np.stack(o, axis=2).reshape(128, -1)
def f(rng, *shape):
    return mx_ref.flush((rng.standard_normal(shape, dtype=np.float32) * np.exp2(rng.integers(-2, 3, shape[:-1] + (1,)))).astype(BF))
def wide(rng, *shape, cols=0):
    v = rng.standard_normal(shape, dtype=np.float32) * np.exp2(rng.integers(-12, 13, shape)).astype(np.float32)
    if cols: v *= np.repeat(np.exp2(rng.integers(-cols, cols + 1, shape[:-2] + (1, shape[-1] // 4))) * (rng.random(shape[:-2] + (1, shape[-1] // 4)) > 0.0625), 4, axis=-1).astype(np.float32)
    return mx_ref.flush(v.astype(BF))
T, L, PL, R = 192, 32, 5, 3
def sized(v, k):
    v = v.astype(np.float32) * np.float32(k)
    v[np.abs(v) < np.float32(2.0 ** -6)] = 0
    return v.astype(BF)
def column(w, k, v):
    w[:, :, 4 * k:4 * k + 4] = np.asarray(v, np.float32).astype(BF)
def plain(rng):
    return {"x": sized(f(rng, N, 128, 4 * T), 16), "w": np.repeat(f(rng, 1, 128, 512), N, axis=0), "z": f(rng, N, 128, 512)}
def setup_inputs(rng):
    return plain(rng)
def setup_inputs_steps(rng):
    d = plain(rng)
    d["w"][:, 96:] = 0
    for t in range(R):
        v = np.zeros((128, 4))
        v[0, 0], v[64, 0] = 1.0, 2.0 ** -21
        column(d["w"], 8 * t + 6, v)
        for i in range(PL): d["w"][:, 64, 4 * (8 * t + i)] = 0
    x = d["x"].reshape(N, 128, T, 4).astype(np.float32)
    x[:, :96] = np.tile(x[:, :96, :T // 4], (1, 1, 4, 1))
    x[:, 64, :, 0] = np.repeat([5.0, 6.0, 7.0, 7.0], T // 4)
    x[:, 0, :, 0] = np.where(np.arange(N) % 2 == 0, 4.0, -4.0)[:, None]
    d["x"] = x.reshape(N, 128, 4 * T).astype(BF)
    return d
def setup_inputs_far(rng):
    d = plain(rng)
    g = 1 - 2 * rng.integers(0, 2, (N, T))
    g[::2] = 1
    v = (1.5 + 0.5 * rng.random((N, 128, 4 * T), dtype=np.float32)) * np.float32(2.0 ** 27)
    d["x"] = (v * np.repeat(g, 4, axis=1)[:, None, :].astype(np.float32)).astype(BF)
    for t in range(R):
        for i in range(PL):
            column(d["w"], 8 * t + i, np.repeat([-1.0, 1.0], 256)[rng.permutation(512)].reshape(128, 4))
        column(d["w"], 8 * t + 6, -(2.0 ** 30) * rng.choice([0.875, 1.0], (128, 4)))
    return d
def setup_inputs_cancel(rng):
    d = plain(rng)
    d["w"][:, 64:] = 0
    d["x"][:, :64, :4] = d["x"][0, :64, :4].astype(np.float32).astype(BF)
    v = rng.integers(4, 8, (64, 4)) * 2.0 ** 22 * rng.choice([-1.0, 1.0], (64, 4))
    k = [1.0, 2.0 ** -26, -1.0, 2.0 ** -26]
    for r in range(N):
        d["x"][r, 64:] = np.tile(v * k[r % 4], (1, T)).astype(np.float32).astype(BF)
    return d
def setup_inputs_bare(rng):
    d = plain(rng)
    a, b = [int(i) for i in rng.permutation(N)[:2]]
    d["x"][:, 127, ::4] = 0
    one = d["x"][a, :, :4].astype(np.float32)
    k = np.repeat(np.exp2(rng.integers(0, 4, T)), 4).astype(np.float32)
    d["x"][a] = (np.tile(one, (1, T)) * k).astype(BF)
    e = np.where(rng.permutation(T) % 4 > 0, -1, np.arange(T))
    d["x"][b] = cols(d["x"][b], e)
    d["x"][b, 127, 4 * np.flatnonzero(e >= 0)] = 65536.0
    for i in range(PL): d["w"][:, 127, 4 * i] = 1.0
    d["w"][:, 127, 4 * 6] = -1.0
    for i in range(PL): column(d["w"], 8 + i, 0)
    column(d["w"], 8 * (R - 1) + 6, 0)
    return d
def setup_inputs_spread(rng):
    return {**plain(rng), "x": sized(wide(rng, N, 128, 4 * T, cols=6), 64)}
def check_inputs(d):
    b = []
    for k, low, high in (("x", 2.0 ** -6, 2.0 ** 28), ("w", 2.0 ** -30, 2.0 ** 30), ("z", 2.0 ** -30, 2.0 ** 30)):
        v = np.abs(d[k].astype(np.float32))
        if not (np.isfinite(v).all() and ((v == 0) | (v >= low) & (v <= high)).all()): b.append("a value of " + k)
    w = d["w"].astype(np.float32)
    if (w != w[:1]).any(): b.append("w differs from rank to rank")
    return b
def reference(x, w, z):
    y, lv = np.zeros((N, 128, T), np.float32), np.zeros((N, R, T), np.float32)
    oc, osc = np.zeros((N, 128, 4 * T), np.uint8), np.zeros((N, 16, T), np.uint8)
    state = [mx_ref.quantize(np.ascontiguousarray(x[r])) for r in range(N)]
    wq = [mx_ref.quantize(np.ascontiguousarray(w[r])) for r in range(N)]
    for t in range(R):
        leaf, have = np.zeros((N, T), int), []
        total = np.zeros((128, L, 4), np.float32)
        for r in range(N):
            p = mx_ref.matmul(wq[r], state[r])[8 * t:8 * t + 7] + np.float32(0)
            have.append(decode(state[r]).reshape(128, T, 4))
            for i in range(PL): leaf[r] += (p[i] < 0) * (1 << i)
            for l in range(L):
                m = np.flatnonzero(leaf[r] == l)
                if m.size: total[:, l] = total[:, l] + have[r][:, m[np.argmax(p[6, m])]]
        v = mx_ref.quantize(np.ascontiguousarray((total * np.float32(0.125)).reshape(128, 4 * L).astype(BF)))
        v = decode(v).reshape(128, L, 4)
        for r in range(N):
            new = have[r] - v[:, leaf[r]] * np.float32(0.5)
            state[r] = mx_ref.quantize(np.ascontiguousarray(new.reshape(128, 4 * T).astype(BF)))
            lv[r, t] = leaf[r]
    for r in range(N):
        y[r] = mx_ref.matmul(mx_ref.quantize(np.ascontiguousarray(z[r])), state[r])
        oc[r], osc[r] = emit(state[r])
    return {"y": y, "oc": oc, "osc": osc, "lv": lv}

@@ -1,0 +1,332 @@
+from concourse.bass import DstId, RemoteDMATransfer
+from concourse.mybir import dt, AluOpType, ActivationFunctionType
+
+NC, L, R = 192, 32, 3
+W = NC + 2
+BIG, MID, LOW = 2.0 ** 96, 2.0 ** 75, 2.0 ** 80
+
+SCRATCH = {
+    "wt": ("sbuf", [128, 128], "bfloat16"), "wb": ("sbuf", [128, 512], "bfloat16"), "zt": ("sbuf", [128, 512], "bfloat16"),
+    "qwb": ("sbuf", [128, 128], "float8_e4m3fn_x4"), "swb": ("sbuf", [128, 128], "uint8"),
+    "qz": ("sbuf", [128, 128], "float8_e4m3fn_x4"), "sz": ("sbuf", [128, 128], "uint8"),
+    "gone": ("sbuf", [128, 520], "bfloat16"), "g1": ("sbuf", [128, 520], "bfloat16"),
+    "g8": ("sbuf", [128, 520], "bfloat16"), "gm": ("sbuf", [128, 520], "bfloat16"),
+    "qe": ("sbuf", [128, 12 * 128], "float8_e4m3fn_x4"), "se": ("sbuf", [128, 12 * 128], "uint8"),
+    "tab": ("sbuf", [128, 32], "bfloat16"), "ones": ("sbuf", [128, 32], "bfloat16"),
+    "i8": ("sbuf", [128, 256], "bfloat16"), "m8": ("sbuf", [128, 256], "bfloat16"), "mh": ("sbuf", [128, NC], "bfloat16"),
+    "i16": ("sbuf", [128, NC], "bfloat16"), "m16": ("sbuf", [128, NC], "bfloat16"),
+    "idg": ("sbuf", [128, NC], "int32"), "idh": ("sbuf", [128, NC], "int32"), "dg": ("sbuf", [128, NC], "bfloat16"),
+    "neg": ("sbuf", [128, W], "bfloat16"),
+    "ip": ("sbuf", [128, 16], "int32"), "ja": ("sbuf", [128, 16], "int32"), "jb": ("sbuf", [128, 16], "int32"),
+    "jc": ("sbuf", [128, 16], "int32"), "jd": ("sbuf", [128, 16], "int32"), "om": ("sbuf", [128, 16], "uint16"),
+    "bt": ("sbuf", [128, NC], "bfloat16"), "btt": ("sbuf", [128, NC], "bfloat16"), "lf": ("sbuf", [128, NC], "bfloat16"),
+    "pn": ("sbuf", [128, NC], "bfloat16"), "pnt": ("sbuf", [128, NC], "bfloat16"),
+    "ky": ("sbuf", [128, W], "float32"), "rm": ("sbuf", [128, W], "float32"), "sg": ("sbuf", [128, NC], "bfloat16"),
+    "ix": ("sbuf", [128, 4], "float32"), "sh": ("sbuf", [128, 32], "bfloat16"), "sht": ("sbuf", [128, 32], "bfloat16"),
+    "shs": ("sbuf", [128, 32], "float32"),
+    "lb": ("sbuf", [128, NC], "bfloat16"), "lt": ("sbuf", [128, NC], "bfloat16"), "ld": ("sbuf", [128, NC], "bfloat16"),
+    "ls": ("sbuf", [128, NC], "float32"), "lvs": ("sbuf", [128, R * NC], "float32"),
+    "vs": ("sbuf", [128, 4 * 256], "float32"), "vt": ("sbuf", [128, 512], "bfloat16"), "ysb": ("sbuf", [128, NC], "float32"),
+    "pb": ("psum", [128, 512], "float32"), "ps": ("psum", [128, 512], "float32"),
+    "pv": ("psum", [128, 1024], "float32"), "px": ("psum", [128, 2048], "float32"),
+}
+for _t in range(R + 1):
+    SCRATCH["h%d" % _t] = ("sbuf", [128, 4 * W], "bfloat16")
+    SCRATCH["qx%d" % _t] = ("sbuf", [128, W], "float8_e4m3fn_x4")
+    SCRATCH["sx%d" % _t] = ("sbuf", [128, W], "uint8")
+for _t in range(R):
+    for _n, _w in (("ws", 128), ("land", 256), ("ql", 256), ("qv", 128), ("vv", NC)):
+        SCRATCH["%s%d" % (_n, _t)] = ("sbuf", [128, _w], "float8_e4m3fn_x4")
+        SCRATCH["%ss%d" % (_n, _t)] = ("sbuf", [128, _w], "uint8")
+    SCRATCH["wl%d" % _t] = ("sbuf", [128, 8], "uint16")
+    SCRATCH["of%d" % _t] = ("sbuf", [128, 2], "uint16")
+    SCRATCH["ov%d" % _t] = ("sbuf", [128, 12], "uint16")
+
+SEMAPHORES = ["cv", "cs", "ct", "cg", "dx", "dw", "dz", "dlv", "dout", "sent"]
+SEMAPHORES += ["plane%d" % _t for _t in range(R)] + ["mate%d" % _t for _t in range(R)]
+
+COUNTER = {"v": "cv", "s": "cs", "t": "ct", "g": "cg"}
+
+
+def _scheduler(g, T):
+    queue = {"v": g.vector, "s": g.scalar, "t": g.tensor, "g": g, "y": g.sync}
+    count = {"cv": 0, "cs": 0, "ct": 0, "cg": 0}
+    clock = {q: {} for q in queue}
+    known = {}
+    writer, readers = {}, {}
+
+    def wait(q, token):
+        name, value = token
+        if clock[q].get(name, 0) >= value:
+            return
+        queue[q].wait_ge(T.sem[name], value)
+        for n, v in list(known.get(token, {}).items()) + [token]:
+            clock[q][n] = max(clock[q].get(n, 0), v)
+
+    def need(q, reads, writes):
+        tokens = {}
+        own = COUNTER.get(q)
+        for k in list(reads) + list(writes):
+            if k in writer:
+                n, v = writer[k]
+                tokens[n] = max(tokens.get(n, 0), v)
+        for k in writes:
+            for n, v in readers.get(k, []):
+                if n != own:
+                    tokens[n] = max(tokens.get(n, 0), v)
+        for n in sorted(tokens):
+            wait(q, (n, tokens[n]))
+
+    def note(q, token, reads, writes):
+        known[token] = dict(clock[q])
+        for k in reads:
+            readers.setdefault(k, []).append(token)
+        for k in writes:
+            writer[k] = token
+            readers[k] = []
+
+    def run(q, reads, writes, call):
+        need(q, reads, writes)
+        name = COUNTER[q]
+        call(queue[q]).then_inc(T.sem[name], 1)
+        count[name] += 1
+        note(q, (name, count[name]), reads, writes)
+
+    def dma(q, sem, value, reads, writes, out, in_):
+        need(q, reads, writes)
+        queue[q].dma_start(out, in_).then_inc(T.sem[sem], 16)
+        note(q, (sem, value), reads, writes)
+
+    def arrive(token, writes):
+        for k in writes:
+            writer[k] = token
+            readers[k] = []
+
+    def finish(q):
+        for name in sorted(count):
+            if count[name]:
+                wait(q, (name, count[name]))
+
+    return run, dma, need, wait, arrive, finish
+
+
+def rank_program(g, core, T, topo):
+    rank = T.rank_of(core)
+    if rank is None:
+        return
+    A, F = AluOpType, ActivationFunctionType
+    run, dma, need, wait, arrive, finish = _scheduler(g, T)
+    u8, u32 = dt.uint8, dt.uint32
+
+    cores = list(T.cores)
+    first = [c for c in cores if c == cores[0] or topo.same_plane(c, cores[0])]
+    planes = [first, [c for c in cores if c not in first]]
+    half = 128
+    at = {}
+    for k, plane in enumerate(planes):
+        for i, c in enumerate(plane):
+            at[cores.index(c)] = half * k + L * i
+    mine = 0 if core in first else 1
+    peers = [c for c in planes[mine] if c != core]
+    mate = [c for c in planes[1 - mine] if topo.mates(c, core)][0]
+    step = [at[1 << k] - at[0] for k in range(3)]
+    for r in range(8):
+        assert at[r] == at[0] + sum(step[k] for k in range(3) if r >> k & 1)
+
+    dma("s", "dw", 16, [], ["wt"], T.wt[:], T.w[:, 0:128])
+    dma("y", "dx", 16, [], ["h0"], T.h0[:, 0:4 * NC], T.x[:])
+    dma("y", "dz", 16, [], ["zt"], T.zt[:], T.z[:])
+    run("g", [], ["tab"], lambda q: q.iota(T.tab[:], [[1, 32]], 0, 0, allow_small_or_imprecise_dtypes=True))
+    run("g", [], ["i8"], lambda q: q.iota(T.i8[:], [[0, 32], [1, 8]], 0, 0, allow_small_or_imprecise_dtypes=True))
+    run("g", [], ["idg"], lambda q: q.iota(T.idg[:], [[1, NC]], 128, -1))
+    run("g", [], ["i16"], lambda q: q.iota(T.i16[:], [[0, 12], [1, 16]], 0, 0, allow_small_or_imprecise_dtypes=True))
+    run("v", [], ["gone"], lambda q: q.memset(T.gone[:], 1.0))
+    run("v", [], ["hp0"], lambda q: q.memset(T.h0[:, 4 * NC:4 * W], 0.0))
+    run("v", [], ["wl0"], lambda q: q.memset(T.wl0[:], 6))
+    run("g", ["gone"], ["g1"], lambda q: q.affine_select(T.g1[:], T.gone[:], [[-1, 520]], A.is_equal, 0.0, 4, 4))
+    run("g", [], ["ip"], lambda q: q.iota(T.ip[:], [[0, 16]], 0, 1))
+    run("g", [], ["ja"], lambda q: q.iota(T.ja[:], [[2, 16]], at[0], 0))
+    run("v", [], ["neg"], lambda q: q.memset(T.neg[:], -BIG))
+    run("v", [], ["kyp"], lambda q: q.memset(T.ky[:, NC:W], -MID))
+    run("v", [], ["ones"], lambda q: q.memset(T.ones[:], 1.0))
+    run("v", ["i8"], ["mh"], lambda q: q.tensor_scalar(T.mh[:], T.i8[:, 0:NC], 0.0, 0.5, A.is_gt, A.mult))
+    for a in range(4):
+        run("v", ["wt"], ["wb%d" % a], lambda q: q.tensor_copy(T.wb[:, 128 * a:128 * a + 128], T.wt[:]))
+    run("v", ["wb0", "wb1", "wb2", "wb3"], ["qwb"], lambda q: q.quantize_mx(T.qwb[:], T.swb[:], T.wb[:]))
+
+    def strength_tile(t):
+        ws, wss, wl = T["ws%d" % t], T["wss%d" % t], T["wl%d" % t]
+        run("s", ["qwb", "wl%d" % t], ["wss%d" % t], lambda q: q.activation(
+            wss[:], T.swb[:].indirect(wl[:]), F.Copy))
+        run("v", ["qwb", "wl%d" % t], ["ws%d" % t], lambda q: q.tensor_copy(
+            ws[:].bitcast(u32), T.qwb[:].bitcast(u32).indirect(wl[:])))
+
+    run("v", ["h0", "hp0"], ["qx0"], lambda q: q.quantize_mx(T.qx0[:], T.sx0[:], T.h0[:]))
+    strength_tile(0)
+    run("v", ["idg"], ["idh"], lambda q: q.tensor_scalar(T.idh[:], T.idg[:], 15, None, A.bitwise_and))
+    run("v", ["idh"], ["dg"], lambda q: q.tensor_scalar(T.dg[:], T.idh[:], 0.0, None, A.is_equal))
+    run("v", ["i16"], ["m16"], lambda q: q.tensor_scalar(T.m16[:], T.i16[:], 0.0, None, A.is_gt))
+
+    def unit_tiles(s, name):
+        src = T[name]
+        for b in range(4):
+            o = 128 * (4 * s + b)
+            run("v", [name], ["e%d%d" % (s, b)], lambda q: q.quantize_mx(
+                T.qe[:, o:o + 128], T.se[:, o:o + 128], src[:, 4 - b:516 - b]))
+
+    def unit(s, b):
+        o = 128 * (4 * s + b)
+        return T.qe[:, o:o + 128], T.se[:, o:o + 128]
+
+    def window_constants(t):
+        if t == 0:
+            unit_tiles(1, "g1")
+            run("v", ["g1"], ["g8"], lambda q: q.tensor_scalar(T.g8[:], T.g1[:], 0.125, None, A.mult))
+            unit_tiles(0, "g8")
+            run("v", ["i8"], ["m8"], lambda q: q.tensor_scalar(T.m8[:], T.i8[:], 0.0, None, A.is_gt))
+            coef = [step[k] / (1 << k) for k in range(3)] + [1 / 8]
+            acc, nxt = "ja", "jd"
+            for k in range(4):
+                a, n = acc, nxt
+                run("v", ["ip"], ["jb"], lambda q: q.tensor_scalar(T.jb[:], T.ip[:], 1 << k, None, A.bitwise_and))
+                run("v", ["jb"], ["jc"], lambda q: q.tensor_scalar(T.jc[:], T.jb[:], float(coef[k]), None, A.mult))
+                run("v", ["jc", a], [n], lambda q: q.tensor_tensor(T[n][:], T[a][:], T.jc[:], A.add))
+                acc, nxt = n, a
+            a = acc
+            run("v", [a], ["om"], lambda q: q.tensor_copy(T.om[:], T[a][:]))
+            run("v", [], ["vtp"], lambda q: q.memset(T.vt[:, 4 * L:512], 0.0))
+            run("v", ["g1"], ["gm"], lambda q: q.tensor_scalar(T.gm[:], T.g1[:], -0.5, None, A.mult))
+            unit_tiles(2, "gm")
+        if t == 1:
+            run("v", ["zt"], ["qz"], lambda q: q.quantize_mx(T.qz[:], T.sz[:], T.zt[:]))
+        if t + 1 < R:
+            run("v", [], ["wl%d" % (t + 1)], lambda q: q.memset(T["wl%d" % (t + 1)][:], 8 * (t + 1) + 6))
+            strength_tile(t + 1)
+        hn = T["h%d" % (t + 1)]
+        run("v", [], ["hp%d" % (t + 1)], lambda q: q.memset(hn[:, 4 * NC:4 * W], 0.0))
+
+    for t in range(R):
+        qx, sx = T["qx%d" % t], T["sx%d" % t]
+        kx = "qx%d" % t
+        land, lands = T["land%d" % t], T["lands%d" % t]
+        run("t", ["qwb", kx], ["pb"], lambda q: q.matmul_mx(
+            T.pb[:, 0:NC], T.qwb[:], T.swb[:], qx[:, 0:NC], sx[:, 0:NC], True, True))
+        run("t", ["ws%d" % t, "wss%d" % t, kx], ["ps"], lambda q: q.matmul_mx(
+            T.ps[:, 0:NC], T["ws%d" % t][:], T["wss%d" % t][:], qx[:, 0:NC], sx[:, 0:NC], True, True))
+        run("v", ["pb"], ["bt"], lambda q: q.tensor_scalar(T.bt[:], T.pb[:, 0:NC], 0.0, 16.0, A.is_lt, A.mult))
+        run("v", ["bt"], ["btt"], lambda q: q.transpose(T.btt[:], T.bt[:]))
+        run("v", ["btt", "mh"], ["lf"], lambda q: q.tensor_tensor_scan(T.lf[:], T.mh[:], T.btt[:], 0.0, A.mult, A.add))
+        leaf = [T.lf[:, 32 * k + 8 * t + 4:32 * k + 8 * t + 5] for k in range(6)]
+        for k in range(6):
+            run("v", ["lf", "tab"], ["pn%d" % k], lambda q: q.tensor_scalar(
+                T.pn[:, 32 * k:32 * k + 32], T.tab[:], leaf[k], -BIG, A.not_equal, A.mult))
+        run("v", ["pn%d" % k for k in range(6)], ["pnt"], lambda q: q.transpose(T.pnt[:], T.pn[:]))
+        run("v", ["ps", "pnt"], ["ky"], lambda q: q.tensor_tensor(T.ky[:, 0:NC], T.ps[:, 0:NC], T.pnt[:], A.add))
+        run("v", ["ky", "kyp", "neg"], ["rm"], lambda q: q.tensor_tensor_scan(
+            T.rm[:], T.ky[:], T.neg[:], -LOW, A.max, A.max))
+        run("s", ["rm"], ["sg", "ix"], lambda q: q.activation(
+            T.sg[:], T.rm[:, 0:NC], F.Sign, bias=T.rm[:, NC:NC + 1], scale=-1.0, accum_out=T.ix[:, 0:1]))
+        run("v", ["ix", "dg"], ["sh"], lambda q: q.tensor_scalar(T.sh[:], T.dg[:, 0:32], T.ix[:, 0:1], None, A.mult))
+        run("v", ["sh"], ["sht"], lambda q: q.transpose(T.sht[:], T.sh[:]))
+        run("v", ["sht", "m16"], ["shs"], lambda q: q.tensor_tensor_scan(
+            T.shs[:], T.m16[:, 0:32], T.sht[:], 0.0, A.mult, A.add))
+        of = T["of%d" % t]
+        run("v", ["shs"], ["of%d" % t], lambda q: q.tensor_copy(of[:], T.shs[:, 15:32:16]))
+        o = at[rank]
+        run("s", [kx, "of%d" % t], ["reps%d" % t], lambda q: q.activation(
+            lands[:, o:o + L], sx[:].indirect(of[:]), F.Copy))
+        run("v", [kx, "of%d" % t], ["rep%d" % t], lambda q: q.tensor_copy(
+            land[:, o:o + L].bitcast(u32), qx[:].bitcast(u32).indirect(of[:])))
+        ids = []
+        for c in peers:
+            rid, pid = topo.addr(c, core)
+            ids.append(DstId(rid=rid, pnc=pid))
+        mask = topo.mask(core, peers[0])
+        need("g", ["rep%d" % t], [])
+        v = land[:, o:o + L].bitcast(u8)
+        g.remote_dma_fused([RemoteDMATransfer(dst_ids=ids, dma_engine_mask=mask, remote_sem=T.sem["plane%d" % t],
+                                              srcs=[v], dsts=[v] * len(ids))], local_sem=T.sem.sent)
+        need("g", ["reps%d" % t], [])
+        v = lands[:, o:o + L]
+        g.remote_dma_fused([RemoteDMATransfer(dst_ids=ids, dma_engine_mask=mask, remote_sem=T.sem["plane%d" % t],
+                                              srcs=[v], dsts=[v] * len(ids))], local_sem=T.sem.sent)
+        n = 2 * len(topo.engines(core, peers[0]))
+        arrive(("plane%d" % t, n * len(peers)), ["planein%d" % t])
+        need("g", ["planein%d" % t], [])
+        rid, pid = topo.addr(mate, core)
+        mask = topo.mask(core, mate)
+        lo = half * mine
+        v = land[:, lo:lo + half].bitcast(u8)
+        g.remote_dma(v, v, T.sem["mate%d" % t], T.sem.sent, pid, rid, mask)
+        v = lands[:, lo:lo + half]
+        g.remote_dma(v, v, T.sem["mate%d" % t], T.sem.sent, pid, rid, mask)
+        arrive(("mate%d" % t, 2 * len(topo.engines(core, mate))), ["matein%d" % t])
+        window_constants(t)
+        for b in range(4):
+            e, es = unit(1, b)
+            run("t", ["e1%d" % b, kx], ["px%d" % b], lambda q: q.matmul_mx(
+                T.px[:, 512 * b:512 * b + NC], e, es, qx[:, 0:NC], sx[:, 0:NC], True, False))
+        for k in range(6):
+            run("v", ["lf", "ones"], ["lb%d" % k], lambda q: q.tensor_scalar(
+                T.lb[:, 32 * k:32 * k + 32], T.ones[:], leaf[k], None, A.mult))
+        run("v", ["lb%d" % k for k in range(6)], ["lt"], lambda q: q.transpose(T.lt[:], T.lb[:]))
+        run("s", ["lt"], ["lvs%d" % t], lambda q: q.activation(T.lvs[0:1, NC * t:NC * t + NC], T.lt[0:1, :], F.Copy))
+        dma("y", "dlv", 16 * (t + 1), ["lvs%d" % t], [], T.lv[t:t + 1, :], T.lvs[0:1, NC * t:NC * t + NC])
+        run("v", ["lt", "dg"], ["ld"], lambda q: q.tensor_tensor(T.ld[:], T.lt[:], T.dg[:], A.mult))
+        run("v", ["ld", "m16"], ["ls"], lambda q: q.tensor_tensor_scan(T.ls[:], T.m16[:], T.ld[:], 0.0, A.mult, A.add))
+        ov = T["ov%d" % t]
+        run("v", ["ls"], ["ov%d" % t], lambda q: q.tensor_copy(ov[:], T.ls[:, 15:NC:16]))
+        ql, qls = T["ql%d" % t], T["qls%d" % t]
+        here = ["planein%d" % t, "matein%d" % t, "om"]
+        run("s", here + ["reps%d" % t], ["qls%d" % t], lambda q: q.activation(
+            qls[:], lands[:].indirect(T.om[:]), F.Copy))
+        run("v", here + ["rep%d" % t], ["ql%d" % t], lambda q: q.tensor_copy(
+            ql[:].bitcast(u32), land[:].bitcast(u32).indirect(T.om[:])))
+        bank = [("pva", T.pv[:, 0:256]), ("pvb", T.pv[:, 512:768]), ("pb", T.pb[:, 0:256]), ("ps", T.ps[:, 0:256])]
+        for b in range(4):
+            e, es = unit(0, b)
+            run("t", ["e0%d" % b, "ql%d" % t, "qls%d" % t], [bank[b][0]], lambda q: q.matmul_mx(
+                bank[b][1], e, es, ql[:], qls[:], True, True))
+        for b in range(4):
+            run("v", [bank[b][0], "m8"], ["vs%d" % b], lambda q: q.tensor_tensor_scan(
+                T.vs[:, 256 * b:256 * b + 256], T.m8[:], bank[b][1], 0.0, A.mult, A.add))
+        for b in range(4):
+            out, in_ = T.vt[:, b:4 * L:4], T.vs[:, 256 * b + 7:256 * b + 256:8]
+            if b < 3:
+                run("s", ["vs%d" % b], ["vt%d" % b], lambda q: q.activation(out, in_, F.Copy))
+            else:
+                run("v", ["vs%d" % b], ["vt%d" % b], lambda q: q.tensor_copy(out, in_))
+        qv, qvs = T["qv%d" % t], T["qvs%d" % t]
+        run("v", ["vt0", "vt1", "vt2", "vt3", "vtp"], ["qv%d" % t], lambda q: q.quantize_mx(qv[:], qvs[:], T.vt[:]))
+        vv, vvs = T["vv%d" % t], T["vvs%d" % t]
+        run("s", ["qv%d" % t, "ov%d" % t], ["vvs%d" % t], lambda q: q.activation(vvs[:], qvs[:].indirect(ov[:]), F.Copy))
+        run("v", ["qv%d" % t, "ov%d" % t], ["vv%d" % t], lambda q: q.tensor_copy(
+            vv[:].bitcast(u32), qv[:].bitcast(u32).indirect(ov[:])))
+        for b in range(4):
+            e, es = unit(2, b)
+            run("t", ["e2%d" % b, "vv%d" % t, "vvs%d" % t], ["px%d" % b], lambda q: q.matmul_mx(
+                T.px[:, 512 * b:512 * b + NC], e, es, vv[:], vvs[:], False, True))
+        hn = T["h%d" % (t + 1)]
+        for b in range(4):
+            out, in_ = hn[:, b:4 * NC:4], T.px[:, 512 * b:512 * b + NC]
+            if b % 2 == 0:
+                run("s", ["px%d" % b], ["h%d%d" % (t + 1, b)], lambda q: q.activation(out, in_, F.Copy))
+            else:
+                run("v", ["px%d" % b], ["h%d%d" % (t + 1, b)], lambda q: q.tensor_copy(out, in_))
+        run("v", ["h%d%d" % (t + 1, b) for b in range(4)] + ["hp%d" % (t + 1)], ["qx%d" % (t + 1)],
+            lambda q: q.quantize_mx(T["qx%d" % (t + 1)][:], T["sx%d" % (t + 1)][:], hn[:]))
+
+    qx, sx = T["qx%d" % R], T["sx%d" % R]
+    kx = "qx%d" % R
+    run("t", ["qz", kx], ["pb"], lambda q: q.matmul_mx(
+        T.pb[:, 0:NC], T.qz[:], T.sz[:], qx[:, 0:NC], sx[:, 0:NC], True, True))
+    total = 16 * 6
+    dma("y", "dout", total, [kx], [], T.oc[:], qx[:, 0:NC].bitcast(u8))
+    for k in range(4):
+        dma("s", "dout", total, [kx], [], T.osc[4 * k:4 * k + 4, :], sx[32 * k:32 * k + 4, 0:NC])
+    run("v", ["pb"], ["ysb"], lambda q: q.tensor_copy(T.ysb[:], T.pb[:, 0:NC]))
+    dma("y", "dout", total, ["ysb"], [], T.y[:], T.ysb[:])
+    wait("g", ("sent", R * 2 * (len(topo.engines(core, peers[0])) + len(topo.engines(core, mate)))))
+    finish("g")
+    wait("g", ("dlv", 16 * R))
+    wait("g", ("dout", total))

@@ -1,49 +1,48 @@
 from concourse.bass import DstId, RemoteDMATransfer
 from concourse.mybir import dt, AluOpType, ActivationFunctionType
 
-NC, L, R = 192, 32, 3
+NC, L, R, PL = 192, 32, 3, 5
 W = NC + 2
-BIG, MID, LOW = 2.0 ** 96, 2.0 ** 75, 2.0 ** 80
+P, FLOOR, NONE, DEEP = 2.0 ** 76, -2.0 ** 74, -2.0 ** 72, -2.0 ** 80
+X4, BF, F32, U8, I32, U16 = "float8_e4m3fn_x4", "bfloat16", "float32", "uint8", "int32", "uint16"
 
 SCRATCH = {
-    "wt": ("sbuf", [128, 128], "bfloat16"), "wb": ("sbuf", [128, 512], "bfloat16"), "zt": ("sbuf", [128, 512], "bfloat16"),
-    "qwb": ("sbuf", [128, 128], "float8_e4m3fn_x4"), "swb": ("sbuf", [128, 128], "uint8"),
-    "qz": ("sbuf", [128, 128], "float8_e4m3fn_x4"), "sz": ("sbuf", [128, 128], "uint8"),
-    "gone": ("sbuf", [128, 520], "bfloat16"), "g1": ("sbuf", [128, 520], "bfloat16"),
-    "g8": ("sbuf", [128, 520], "bfloat16"), "gm": ("sbuf", [128, 520], "bfloat16"),
-    "qe": ("sbuf", [128, 12 * 128], "float8_e4m3fn_x4"), "se": ("sbuf", [128, 12 * 128], "uint8"),
-    "tab": ("sbuf", [128, 32], "bfloat16"), "ones": ("sbuf", [128, 32], "bfloat16"),
-    "i8": ("sbuf", [128, 256], "bfloat16"), "m8": ("sbuf", [128, 256], "bfloat16"), "mh": ("sbuf", [128, NC], "bfloat16"),
-    "i16": ("sbuf", [128, NC], "bfloat16"), "m16": ("sbuf", [128, NC], "bfloat16"),
-    "idg": ("sbuf", [128, NC], "int32"), "idh": ("sbuf", [128, NC], "int32"), "dg": ("sbuf", [128, NC], "bfloat16"),
-    "neg": ("sbuf", [128, W], "bfloat16"),
-    "ip": ("sbuf", [128, 16], "int32"), "ja": ("sbuf", [128, 16], "int32"), "jb": ("sbuf", [128, 16], "int32"),
-    "jc": ("sbuf", [128, 16], "int32"), "jd": ("sbuf", [128, 16], "int32"), "om": ("sbuf", [128, 16], "uint16"),
-    "bt": ("sbuf", [128, NC], "bfloat16"), "btt": ("sbuf", [128, NC], "bfloat16"), "lf": ("sbuf", [128, NC], "bfloat16"),
-    "pn": ("sbuf", [128, NC], "bfloat16"), "pnt": ("sbuf", [128, NC], "bfloat16"),
-    "ky": ("sbuf", [128, W], "float32"), "rm": ("sbuf", [128, W], "float32"), "sg": ("sbuf", [128, NC], "bfloat16"),
-    "ix": ("sbuf", [128, 4], "float32"), "sh": ("sbuf", [128, 32], "bfloat16"), "sht": ("sbuf", [128, 32], "bfloat16"),
-    "shs": ("sbuf", [128, 32], "float32"),
-    "lb": ("sbuf", [128, NC], "bfloat16"), "lt": ("sbuf", [128, NC], "bfloat16"), "ld": ("sbuf", [128, NC], "bfloat16"),
-    "ls": ("sbuf", [128, NC], "float32"), "lvs": ("sbuf", [128, R * NC], "float32"),
-    "vs": ("sbuf", [128, 4 * 256], "float32"), "vt": ("sbuf", [128, 512], "bfloat16"), "ysb": ("sbuf", [128, NC], "float32"),
-    "pb": ("psum", [128, 512], "float32"), "ps": ("psum", [128, 512], "float32"),
-    "pv": ("psum", [128, 1024], "float32"), "px": ("psum", [128, 2048], "float32"),
+    "wb": ("sbuf", [128, 576], BF), "zt": ("sbuf", [128, 512], BF),
+    "qwb": ("sbuf", [128, 144], X4), "swb": ("sbuf", [128, 144], U8),
+    "qz": ("sbuf", [128, 128], X4), "sz": ("sbuf", [128, 128], U8),
+    "gone": ("sbuf", [128, 520], BF), "g1": ("sbuf", [128, 520], BF), "g8": ("sbuf", [128, 520], BF),
+    "gm": ("sbuf", [128, 520], BF),
+    "qe": ("sbuf", [128, 12 * 128], X4), "se": ("sbuf", [128, 12 * 128], U8),
+    "u": ("sbuf", [128, 128], BF), "ut": ("sbuf", [128, 128], BF), "gk": ("sbuf", [128, 512], BF),
+    "qc": ("sbuf", [128, 3 * 128], X4), "sc": ("sbuf", [128, 3 * 128], U8),
+    "bq": ("sbuf", [128, 4 * W], BF), "qb": ("sbuf", [128, W], X4), "sb": ("sbuf", [128, W], U8),
+    "m8": ("sbuf", [128, 256], BF), "m16": ("sbuf", [128, NC], BF),
+    "idg": ("sbuf", [128, NC], I32), "idh": ("sbuf", [128, NC], I32), "dg": ("sbuf", [128, NC], BF),
+    "neg": ("sbuf", [128, W], BF),
+    "ip": ("sbuf", [128, 8], I32), "jb": ("sbuf", [128, 16], I32), "ja": ("sbuf", [128, 8], I32),
+    "ik": ("sbuf", [128, 8], I32), "jc": ("sbuf", [128, 8], I32), "jd": ("sbuf", [128, 8], I32),
+    "je": ("sbuf", [128, 8], I32), "jf": ("sbuf", [128, 8], I32), "om": ("sbuf", [128, 8], U16),
+    "rm0": ("sbuf", [128, W], F32), "rm1": ("sbuf", [128, W], F32),
+    "sg0": ("sbuf", [128, NC], BF), "sg1": ("sbuf", [128, NC], BF), "ix": ("sbuf", [128, 4], F32),
+    "lt": ("sbuf", [128, NC], BF), "ld": ("sbuf", [128, NC], BF), "ls": ("sbuf", [128, NC], F32),
+    "lvs": ("sbuf", [128, R * NC], F32),
+    "va": ("sbuf", [128, 1024], BF), "vs": ("sbuf", [128, 1024], BF), "ysb": ("sbuf", [128, NC], F32),
+    "pv": ("psum", [128, 2048], F32), "px": ("psum", [128, 2048], F32),
 }
 for _t in range(R + 1):
-    SCRATCH["h%d" % _t] = ("sbuf", [128, 4 * W], "bfloat16")
-    SCRATCH["qx%d" % _t] = ("sbuf", [128, W], "float8_e4m3fn_x4")
-    SCRATCH["sx%d" % _t] = ("sbuf", [128, W], "uint8")
+    SCRATCH["h%d" % _t] = ("sbuf", [128, 4 * W], BF)
+    SCRATCH["qx%d" % _t] = ("sbuf", [128, W], X4)
+    SCRATCH["sx%d" % _t] = ("sbuf", [128, W], U8)
 for _t in range(R):
-    for _n, _w in (("ws", 128), ("land", 256), ("ql", 256), ("qv", 128), ("vv", NC)):
-        SCRATCH["%s%d" % (_n, _t)] = ("sbuf", [128, _w], "float8_e4m3fn_x4")
-        SCRATCH["%ss%d" % (_n, _t)] = ("sbuf", [128, _w], "uint8")
-    SCRATCH["wl%d" % _t] = ("sbuf", [128, 8], "uint16")
-    SCRATCH["of%d" % _t] = ("sbuf", [128, 2], "uint16")
-    SCRATCH["ov%d" % _t] = ("sbuf", [128, 12], "uint16")
+    for _n, _w in (("ws", 128), ("la", 128), ("lb", 128), ("qa", 128), ("qm", 128), ("qv", 256), ("vv", NC)):
+        SCRATCH["%s%d" % (_n, _t)] = ("sbuf", [128, _w], X4)
+        SCRATCH["%ss%d" % (_n, _t)] = ("sbuf", [128, _w], U8)
+    SCRATCH["wl%d" % _t] = ("sbuf", [128, 8], U16)
+    SCRATCH["of%d" % _t] = ("sbuf", [128, 2], U16)
+    SCRATCH["ov%d" % _t] = ("sbuf", [128, 12], U16)
 
 SEMAPHORES = ["cv", "cs", "ct", "cg", "dx", "dw", "dz", "dlv", "dout", "sent"]
-SEMAPHORES += ["plane%d" % _t for _t in range(R)] + ["mate%d" % _t for _t in range(R)]
+SEMAPHORES += ["%s%d" % (_n, _t) for _n in ("planec", "planes", "matec", "mates") for _t in range(R)]
 
 COUNTER = {"v": "cv", "s": "cs", "t": "ct", "g": "cg"}
 
@@ -121,38 +120,59 @@ def rank_program(g, core, T, topo):
     cores = list(T.cores)
     first = [c for c in cores if c == cores[0] or topo.same_plane(c, cores[0])]
     planes = [first, [c for c in cores if c not in first]]
-    half = 128
-    at = {}
-    for k, plane in enumerate(planes):
-        for i, c in enumerate(plane):
-            at[cores.index(c)] = half * k + L * i
     mine = 0 if core in first else 1
+    me = planes[mine].index(core)
+    mate = planes[1 - mine][me]
+    assert topo.mates(core, mate)
+    for a in range(2):
+        for i in range(4):
+            assert planes[a][i] == cores[2 * i + a]
     peers = [c for c in planes[mine] if c != core]
-    mate = [c for c in planes[1 - mine] if topo.mates(c, core)][0]
-    step = [at[1 << k] - at[0] for k in range(3)]
-    for r in range(8):
-        assert at[r] == at[0] + sum(step[k] for k in range(3) if r >> k & 1)
 
-    dma("s", "dw", 16, [], ["wt"], T.wt[:], T.w[:, 0:128])
+    def bank(b, n):
+        return T.pv[:, 512 * b:512 * b + n]
+
+    dma("s", "dw", 16, [], ["wb"], T.wb[:, 0:128], T.w[:, 0:128])
     dma("y", "dx", 16, [], ["h0"], T.h0[:, 0:4 * NC], T.x[:])
     dma("y", "dz", 16, [], ["zt"], T.zt[:], T.z[:])
-    run("g", [], ["tab"], lambda q: q.iota(T.tab[:], [[1, 32]], 0, 0, allow_small_or_imprecise_dtypes=True))
-    run("g", [], ["i8"], lambda q: q.iota(T.i8[:], [[0, 32], [1, 8]], 0, 0, allow_small_or_imprecise_dtypes=True))
-    run("g", [], ["idg"], lambda q: q.iota(T.idg[:], [[1, NC]], 128, -1))
-    run("g", [], ["i16"], lambda q: q.iota(T.i16[:], [[0, 12], [1, 16]], 0, 0, allow_small_or_imprecise_dtypes=True))
-    run("v", [], ["gone"], lambda q: q.memset(T.gone[:], 1.0))
-    run("v", [], ["hp0"], lambda q: q.memset(T.h0[:, 4 * NC:4 * W], 0.0))
+    run("g", [], ["ip"], lambda q: q.iota(T.ip[:], [[0, 8]], 0, 1))
+    run("g", [], ["bqc"], lambda q: q.iota(T.bq[:], [[0, 4 * W]], 1, 0, allow_small_or_imprecise_dtypes=True))
+    run("g", ["bqc"], ["bqp"], lambda q: q.iota(
+        T.bq[:, 4 * NC:4 * W], [[0, 4 * W - 4 * NC]], 2, 0, allow_small_or_imprecise_dtypes=True))
+    run("v", [], ["wbz"], lambda q: q.memset(T.wb[:, 128:576], 0.0))
     run("v", [], ["wl0"], lambda q: q.memset(T.wl0[:], 6))
+    run("v", [], ["hp0"], lambda q: q.memset(T.h0[:, 4 * NC:4 * W], 0.0))
+    run("v", [], ["gone"], lambda q: q.memset(T.gone[:], 1.0))
     run("g", ["gone"], ["g1"], lambda q: q.affine_select(T.g1[:], T.gone[:], [[-1, 520]], A.is_equal, 0.0, 4, 4))
-    run("g", [], ["ip"], lambda q: q.iota(T.ip[:], [[0, 16]], 0, 1))
-    run("g", [], ["ja"], lambda q: q.iota(T.ja[:], [[2, 16]], at[0], 0))
-    run("v", [], ["neg"], lambda q: q.memset(T.neg[:], -BIG))
-    run("v", [], ["kyp"], lambda q: q.memset(T.ky[:, NC:W], -MID))
-    run("v", [], ["ones"], lambda q: q.memset(T.ones[:], 1.0))
-    run("v", ["i8"], ["mh"], lambda q: q.tensor_scalar(T.mh[:], T.i8[:, 0:NC], 0.0, 0.5, A.is_gt, A.mult))
-    for a in range(4):
-        run("v", ["wt"], ["wb%d" % a], lambda q: q.tensor_copy(T.wb[:, 128 * a:128 * a + 128], T.wt[:]))
-    run("v", ["wb0", "wb1", "wb2", "wb3"], ["qwb"], lambda q: q.quantize_mx(T.qwb[:], T.swb[:], T.wb[:]))
+    run("g", [], ["ja"], lambda q: q.iota(T.ja[:], [[4, 8]], 0, 0))
+    run("g", [], ["ik"], lambda q: q.iota(T.ik[:], [[0, 8]], L * (4 - me), L))
+    run("g", [], ["idg"], lambda q: q.iota(T.idg[:], [[1, NC]], 128, -1))
+
+    def laid(k):
+        run("v", ["u", "u0", "u1", "u2", "u3", "u4"], ["ut"], lambda q: q.transpose(T.ut[:], T.u[:]))
+        run("v", ["ut", "gkz"], ["gk0"], lambda q: q.tensor_copy(T.gk[:, 0:512:4], T.ut[:]))
+        run("v", ["gk0", "gk1", "gkz"], ["qc%d" % k], lambda q: q.quantize_mx(
+            T.qc[:, 128 * k:128 * k + 128], T.sc[:, 128 * k:128 * k + 128], T.gk[:]))
+
+    def const(k):
+        return T.qc[:, 128 * k:128 * k + 128], T.sc[:, 128 * k:128 * k + 128]
+
+    run("v", [], ["u"], lambda q: q.memset(T.u[:], 0.0))
+    run("v", [], ["gkz"], lambda q: q.memset(T.gk[:], 0.0))
+    for i in range(PL - 1):
+        run("v", ["ip"], ["jb%d" % i], lambda q: q.tensor_scalar(
+            T.jb[0:32, 4 * i:4 * i + 4], T.ip[0:32, 0:4], 1 << i, None, A.bitwise_and))
+    for i in range(PL - 1):
+        run("v", ["jb%d" % i, "u"], ["u%d" % i], lambda q: q.tensor_scalar(
+            T.u[0:32, i:128:32], T.jb[0:32, 4 * i:4 * i + 4], 2 * P / (1 << i), P, A.mult, A.subtract))
+    run("v", ["u"], ["u4"], lambda q: q.memset(T.u[0:32, 4:128:32], -P))
+    run("v", ["gkz"], ["gk1"], lambda q: q.memset(T.gk[:, 1:512:4], -P * PL / 2 / 128))
+    laid(0)
+    run("v", ["u"], ["u4"], lambda q: q.memset(T.u[0:32, 4:128:32], P))
+    laid(1)
+    run("v", [], ["neg"], lambda q: q.memset(T.neg[:], DEEP))
+    run("v", ["neg"], ["negp"], lambda q: q.memset(T.neg[:, NC:W], NONE))
+    run("v", ["wb", "wbz"], ["qwb"], lambda q: q.quantize_mx(T.qwb[:], T.swb[:], T.wb[:]))
 
     def strength_tile(t):
         ws, wss, wl = T["ws%d" % t], T["wss%d" % t], T["wl%d" % t]
@@ -161,11 +181,8 @@ def rank_program(g, core, T, topo):
         run("v", ["qwb", "wl%d" % t], ["ws%d" % t], lambda q: q.tensor_copy(
             ws[:].bitcast(u32), T.qwb[:].bitcast(u32).indirect(wl[:])))
 
-    run("v", ["h0", "hp0"], ["qx0"], lambda q: q.quantize_mx(T.qx0[:], T.sx0[:], T.h0[:]))
     strength_tile(0)
-    run("v", ["idg"], ["idh"], lambda q: q.tensor_scalar(T.idh[:], T.idg[:], 15, None, A.bitwise_and))
-    run("v", ["idh"], ["dg"], lambda q: q.tensor_scalar(T.dg[:], T.idh[:], 0.0, None, A.is_equal))
-    run("v", ["i16"], ["m16"], lambda q: q.tensor_scalar(T.m16[:], T.i16[:], 0.0, None, A.is_gt))
+    run("v", ["h0", "hp0"], ["qx0"], lambda q: q.quantize_mx(T.qx0[:], T.sx0[:], T.h0[:]))
 
     def unit_tiles(s, name):
         src = T[name]
@@ -178,24 +195,126 @@ def rank_program(g, core, T, topo):
         o = 128 * (4 * s + b)
         return T.qe[:, o:o + 128], T.se[:, o:o + 128]
 
-    def window_constants(t):
+    def first_constants():
+        unit_tiles(1, "g1")
+        run("s", ["g1"], ["g8"], lambda q: q.activation(T.g8[:], T.g1[:], F.Copy, scale=0.125))
+        run("s", ["g1"], ["gm"], lambda q: q.activation(T.gm[:], T.g1[:], F.Copy, scale=-0.5))
+        run("v", [], ["u"], lambda q: q.memset(T.u[:], 0.0))
+        for i in range(PL):
+            run("v", ["u"], ["u%d" % i], lambda q: q.memset(T.u[0:32, i:128:32], 2.0 ** i))
+        run("v", ["gkz"], ["gk1"], lambda q: q.memset(T.gk[:, 1:512:4], 0.0))
+        laid(2)
+        run("v", ["idg"], ["idh"], lambda q: q.tensor_scalar(T.idh[:], T.idg[:], 15, None, A.bitwise_and))
+        run("v", [], ["m16"], lambda q: q.memset(T.m16[:], 1.0))
+        run("v", ["idh"], ["dg"], lambda q: q.tensor_scalar(T.dg[:], T.idh[:], 0.0, None, A.is_equal))
+        run("v", ["m16"], ["m16z"], lambda q: q.memset(T.m16[:, 0:NC:16], 0.0))
+        run("v", ["ip"], ["jc"], lambda q: q.tensor_scalar(
+            T.jc[:], T.ip[:], 2, 3, A.arith_shift_right, A.bitwise_and))
+        run("v", ["ik"], ["jd"], lambda q: q.tensor_scalar(T.jd[:], T.ik[:], 3 * L, None, A.bitwise_and))
+        run("v", ["jc", "ja"], ["je"], lambda q: q.tensor_tensor(T.je[:], T.ja[:], T.jc[:], A.add))
+        run("v", [], ["m8"], lambda q: q.memset(T.m8[:], 1.0))
+        run("v", ["jd", "je"], ["jf"], lambda q: q.tensor_tensor(T.jf[:], T.je[:], T.jd[:], A.add))
+        run("v", ["m8"], ["m8z"], lambda q: q.memset(T.m8[:, 0:256:8], 0.0))
+        run("v", ["jf"], ["om"], lambda q: q.tensor_copy(T.om[:], T.jf[:]))
+
+    half = (2 ** PL - 1) / 2
+    for t in range(R):
+        qx, sx = T["qx%d" % t], T["sx%d" % t]
+        kx = "qx%d" % t
+        la, las, lb, lbs = T["la%d" % t], T["las%d" % t], T["lb%d" % t], T["lbs%d" % t]
+        run("t", ["qwb", kx], ["b0"], lambda q: q.matmul_mx(
+            bank(0, W), T.qwb[:, 8 * t:8 * t + 128], T.swb[:, 8 * t:8 * t + 128], qx[:], sx[:], True, True))
+        for c in range(2):
+            run("t", ["ws%d" % t, "wss%d" % t, kx], ["b%d" % (1 + c)], lambda q: q.matmul_mx(
+                bank(1 + c, W), T["ws%d" % t][:], T["wss%d" % t][:], qx[:], sx[:], True, False))
+        run("v", ["b0", "bqc", "bqp"], ["bq"], lambda q: q.tensor_scalar(
+            T.bq[:, 0:4 * W:4], bank(0, W), 0.0, 0.5, A.is_lt, A.subtract))
+        run("v", ["bq"], ["qb"], lambda q: q.quantize_mx(T.qb[:], T.sb[:], T.bq[:]))
+        for c in range(2):
+            e, es = const(c)
+            run("t", ["qc%d" % c, "qb"], ["b%d" % (1 + c)], lambda q: q.matmul_mx(
+                bank(1 + c, W), e, es, T.qb[:], T.sb[:], False, True))
+        for c in range(2):
+            rm, sg = T["rm%d" % c], T["sg%d" % c]
+            run("v", ["b%d" % (1 + c), "neg", "negp"], ["rm%d" % c], lambda q: q.tensor_tensor_scan(
+                rm[:], bank(1 + c, W), T.neg[:], FLOOR, A.max, A.max))
+            run("s", ["rm%d" % c], ["sg%d" % c, "ix%d" % c], lambda q: q.activation(
+                sg[:], rm[:, 0:NC], F.Sign, bias=rm[:, NC:NC + 1], scale=-1.0, accum_out=T.ix[:, c:c + 1]))
+        of = T["of%d" % t]
+        run("v", ["ix0", "ix1"], ["of%d" % t], lambda q: q.tensor_copy(of[:], T.ix[:, 0:2]))
+        run("s", [kx, "of%d" % t], ["reps%d" % t], lambda q: q.activation(
+            las[:, 0:L], sx[:].indirect(of[:]), F.Copy))
+        run("v", [kx, "of%d" % t], ["rep%d" % t], lambda q: q.tensor_copy(
+            la[:, 0:L].bitcast(u32), qx[:].bitcast(u32).indirect(of[:])))
+        ids, slot = [], []
+        for c in peers:
+            rid, pid = topo.addr(c, core)
+            ids.append(DstId(rid=rid, pnc=pid))
+            slot.append(L * ((me - planes[mine].index(c)) % 4))
+        mask = topo.mask(core, peers[0])
+        need("g", ["rep%d" % t], [])
+        g.remote_dma_fused([RemoteDMATransfer(
+            dst_ids=ids, dma_engine_mask=mask, remote_sem=T.sem["planec%d" % t], srcs=[la[:, 0:L].bitcast(u8)],
+            dsts=[la[:, o:o + L].bitcast(u8) for o in slot])], local_sem=T.sem.sent)
+        need("g", ["reps%d" % t], [])
+        g.remote_dma_fused([RemoteDMATransfer(
+            dst_ids=ids, dma_engine_mask=mask, remote_sem=T.sem["planes%d" % t], srcs=[las[:, 0:L]],
+            dsts=[las[:, o:o + L] for o in slot])], local_sem=T.sem.sent)
+        n = len(topo.engines(core, peers[0])) * len(peers)
+        arrive(("planec%d" % t, n), ["pc%d" % t])
+        arrive(("planes%d" % t, n), ["ps%d" % t])
+        rid, pid = topo.addr(mate, core)
+        mask = topo.mask(core, mate)
+        mc, ms = T.sem["matec%d" % t], T.sem["mates%d" % t]
+        g.remote_dma(lb[:, 0:L].bitcast(u8), la[:, 0:L].bitcast(u8), mc, T.sem.sent, pid, rid, mask)
+        g.remote_dma(lbs[:, 0:L], las[:, 0:L], ms, T.sem.sent, pid, rid, mask)
+        need("g", ["pc%d" % t], [])
+        g.remote_dma(lb[:, L:4 * L].bitcast(u8), la[:, L:4 * L].bitcast(u8), mc, T.sem.sent, pid, rid, mask)
+        need("g", ["ps%d" % t], [])
+        g.remote_dma(lbs[:, L:4 * L], las[:, L:4 * L], ms, T.sem.sent, pid, rid, mask)
+        n = 2 * len(topo.engines(core, mate))
+        arrive(("matec%d" % t, n), ["mc%d" % t])
+        arrive(("mates%d" % t, n), ["ms%d" % t])
         if t == 0:
-            unit_tiles(1, "g1")
-            run("v", ["g1"], ["g8"], lambda q: q.tensor_scalar(T.g8[:], T.g1[:], 0.125, None, A.mult))
+            first_constants()
+        e, es = const(2)
+        run("t", ["qc2", "qb"], ["b3"], lambda q: q.matmul_mx(
+            bank(3, NC), e, es, T.qb[:, 0:NC], T.sb[:, 0:NC], True, True))
+        for b in range(4):
+            e, es = unit(1, b)
+            run("t", ["e1%d" % b, kx], ["px%d" % b], lambda q: q.matmul_mx(
+                T.px[:, 512 * b:512 * b + NC], e, es, qx[:, 0:NC], sx[:, 0:NC], True, False))
+        run("s", ["b3"], ["lt"], lambda q: q.activation(T.lt[:], bank(3, NC), F.Copy))
+        run("s", ["b3"], ["lvs%d" % t], lambda q: q.activation(
+            T.lvs[0:1, NC * t:NC * t + NC], T.pv[0:1, 3 * 512:3 * 512 + NC], F.Identity, bias=half))
+        dma("y", "dlv", 16 * (t + 1), ["lvs%d" % t], [], T.lv[t:t + 1, :], T.lvs[0:1, NC * t:NC * t + NC])
+        run("v", ["lt", "dg"], ["ld"], lambda q: q.tensor_tensor(T.ld[:], T.lt[:], T.dg[:], A.mult))
+        run("v", ["ld", "m16", "m16z"], ["ls"], lambda q: q.tensor_tensor_scan(
+            T.ls[:], T.m16[:], T.ld[:], 0.0, A.mult, A.add))
+        ov = T["ov%d" % t]
+        run("v", ["ls"], ["ov%d" % t], lambda q: q.tensor_scalar(
+            ov[:], T.ls[:, 15:NC:16], 8.0, 8.0 * half + 7.0, A.mult, A.add))
+        if t == 0:
             unit_tiles(0, "g8")
-            run("v", ["i8"], ["m8"], lambda q: q.tensor_scalar(T.m8[:], T.i8[:], 0.0, None, A.is_gt))
-            coef = [step[k] / (1 << k) for k in range(3)] + [1 / 8]
-            acc, nxt = "ja", "jd"
-            for k in range(4):
-                a, n = acc, nxt
-                run("v", ["ip"], ["jb"], lambda q: q.tensor_scalar(T.jb[:], T.ip[:], 1 << k, None, A.bitwise_and))
-                run("v", ["jb"], ["jc"], lambda q: q.tensor_scalar(T.jc[:], T.jb[:], float(coef[k]), None, A.mult))
-                run("v", ["jc", a], [n], lambda q: q.tensor_tensor(T[n][:], T[a][:], T.jc[:], A.add))
-                acc, nxt = n, a
-            a = acc
-            run("v", [a], ["om"], lambda q: q.tensor_copy(T.om[:], T[a][:]))
-            run("v", [], ["vtp"], lambda q: q.memset(T.vt[:, 4 * L:512], 0.0))
-            run("v", ["g1"], ["gm"], lambda q: q.tensor_scalar(T.gm[:], T.g1[:], -0.5, None, A.mult))
+
+        def plane_values(src, srcs, out, outs, kq, kc, ks, a, engine):
+            run("v", kc + ["om"], [kq], lambda q: q.tensor_copy(
+                out[:].bitcast(u32), src[:].bitcast(u32).indirect(T.om[:])))
+            run("s", ks + ["om"], [kq + "s"], lambda q: q.activation(outs[:], srcs[:].indirect(T.om[:]), F.Copy))
+            for b in range(4):
+                e, es = unit(0, b)
+                run("t", ["e0%d" % b, kq, kq + "s"], ["b%d" % b], lambda q: q.matmul_mx(
+                    bank(b, 4 * L), e, es, out[:], outs[:], True, True))
+            for b in range(4):
+                place = T.va[:, 256 * b + a:256 * b + 256:2]
+                if engine[b] == "s":
+                    run("s", ["b%d" % b], ["va%d%d" % (b, a)], lambda q: q.activation(place, bank(b, 4 * L), F.Copy))
+                else:
+                    run("v", ["b%d" % b], ["va%d%d" % (b, a)], lambda q: q.tensor_copy(place, bank(b, 4 * L)))
+
+        plane_values(la, las, T["qa%d" % t], T["qas%d" % t], "qa%d" % t, ["rep%d" % t, "pc%d" % t],
+                     ["reps%d" % t, "ps%d" % t], mine, "ssss")
+        if t == 0:
             unit_tiles(2, "gm")
         if t == 1:
             run("v", ["zt"], ["qz"], lambda q: q.quantize_mx(T.qz[:], T.sz[:], T.zt[:]))
@@ -204,100 +323,12 @@ def rank_program(g, core, T, topo):
             strength_tile(t + 1)
         hn = T["h%d" % (t + 1)]
         run("v", [], ["hp%d" % (t + 1)], lambda q: q.memset(hn[:, 4 * NC:4 * W], 0.0))
-
-    for t in range(R):
-        qx, sx = T["qx%d" % t], T["sx%d" % t]
-        kx = "qx%d" % t
-        land, lands = T["land%d" % t], T["lands%d" % t]
-        run("t", ["qwb", kx], ["pb"], lambda q: q.matmul_mx(
-            T.pb[:, 0:NC], T.qwb[:], T.swb[:], qx[:, 0:NC], sx[:, 0:NC], True, True))
-        run("t", ["ws%d" % t, "wss%d" % t, kx], ["ps"], lambda q: q.matmul_mx(
-            T.ps[:, 0:NC], T["ws%d" % t][:], T["wss%d" % t][:], qx[:, 0:NC], sx[:, 0:NC], True, True))
-        run("v", ["pb"], ["bt"], lambda q: q.tensor_scalar(T.bt[:], T.pb[:, 0:NC], 0.0, 16.0, A.is_lt, A.mult))
-        run("v", ["bt"], ["btt"], lambda q: q.transpose(T.btt[:], T.bt[:]))
-        run("v", ["btt", "mh"], ["lf"], lambda q: q.tensor_tensor_scan(T.lf[:], T.mh[:], T.btt[:], 0.0, A.mult, A.add))
-        leaf = [T.lf[:, 32 * k + 8 * t + 4:32 * k + 8 * t + 5] for k in range(6)]
-        for k in range(6):
-            run("v", ["lf", "tab"], ["pn%d" % k], lambda q: q.tensor_scalar(
-                T.pn[:, 32 * k:32 * k + 32], T.tab[:], leaf[k], -BIG, A.not_equal, A.mult))
-        run("v", ["pn%d" % k for k in range(6)], ["pnt"], lambda q: q.transpose(T.pnt[:], T.pn[:]))
-        run("v", ["ps", "pnt"], ["ky"], lambda q: q.tensor_tensor(T.ky[:, 0:NC], T.ps[:, 0:NC], T.pnt[:], A.add))
-        run("v", ["ky", "kyp", "neg"], ["rm"], lambda q: q.tensor_tensor_scan(
-            T.rm[:], T.ky[:], T.neg[:], -LOW, A.max, A.max))
-        run("s", ["rm"], ["sg", "ix"], lambda q: q.activation(
-            T.sg[:], T.rm[:, 0:NC], F.Sign, bias=T.rm[:, NC:NC + 1], scale=-1.0, accum_out=T.ix[:, 0:1]))
-        run("v", ["ix", "dg"], ["sh"], lambda q: q.tensor_scalar(T.sh[:], T.dg[:, 0:32], T.ix[:, 0:1], None, A.mult))
-        run("v", ["sh"], ["sht"], lambda q: q.transpose(T.sht[:], T.sh[:]))
-        run("v", ["sht", "m16"], ["shs"], lambda q: q.tensor_tensor_scan(
-            T.shs[:], T.m16[:, 0:32], T.sht[:], 0.0, A.mult, A.add))
-        of = T["of%d" % t]
-        run("v", ["shs"], ["of%d" % t], lambda q: q.tensor_copy(of[:], T.shs[:, 15:32:16]))
-        o = at[rank]
-        run("s", [kx, "of%d" % t], ["reps%d" % t], lambda q: q.activation(
-            lands[:, o:o + L], sx[:].indirect(of[:]), F.Copy))
-        run("v", [kx, "of%d" % t], ["rep%d" % t], lambda q: q.tensor_copy(
-            land[:, o:o + L].bitcast(u32), qx[:].bitcast(u32).indirect(of[:])))
-        ids = []
-        for c in peers:
-            rid, pid = topo.addr(c, core)
-            ids.append(DstId(rid=rid, pnc=pid))
-        mask = topo.mask(core, peers[0])
-        need("g", ["rep%d" % t], [])
-        v = land[:, o:o + L].bitcast(u8)
-        g.remote_dma_fused([RemoteDMATransfer(dst_ids=ids, dma_engine_mask=mask, remote_sem=T.sem["plane%d" % t],
-                                              srcs=[v], dsts=[v] * len(ids))], local_sem=T.sem.sent)
-        need("g", ["reps%d" % t], [])
-        v = lands[:, o:o + L]
-        g.remote_dma_fused([RemoteDMATransfer(dst_ids=ids, dma_engine_mask=mask, remote_sem=T.sem["plane%d" % t],
-                                              srcs=[v], dsts=[v] * len(ids))], local_sem=T.sem.sent)
-        n = 2 * len(topo.engines(core, peers[0]))
-        arrive(("plane%d" % t, n * len(peers)), ["planein%d" % t])
-        need("g", ["planein%d" % t], [])
-        rid, pid = topo.addr(mate, core)
-        mask = topo.mask(core, mate)
-        lo = half * mine
-        v = land[:, lo:lo + half].bitcast(u8)
-        g.remote_dma(v, v, T.sem["mate%d" % t], T.sem.sent, pid, rid, mask)
-        v = lands[:, lo:lo + half]
-        g.remote_dma(v, v, T.sem["mate%d" % t], T.sem.sent, pid, rid, mask)
-        arrive(("mate%d" % t, 2 * len(topo.engines(core, mate))), ["matein%d" % t])
-        window_constants(t)
+        plane_values(lb, lbs, T["qm%d" % t], T["qms%d" % t], "qm%d" % t, ["mc%d" % t], ["ms%d" % t], 1 - mine, "vsss")
         for b in range(4):
-            e, es = unit(1, b)
-            run("t", ["e1%d" % b, kx], ["px%d" % b], lambda q: q.matmul_mx(
-                T.px[:, 512 * b:512 * b + NC], e, es, qx[:, 0:NC], sx[:, 0:NC], True, False))
-        for k in range(6):
-            run("v", ["lf", "ones"], ["lb%d" % k], lambda q: q.tensor_scalar(
-                T.lb[:, 32 * k:32 * k + 32], T.ones[:], leaf[k], None, A.mult))
-        run("v", ["lb%d" % k for k in range(6)], ["lt"], lambda q: q.transpose(T.lt[:], T.lb[:]))
-        run("s", ["lt"], ["lvs%d" % t], lambda q: q.activation(T.lvs[0:1, NC * t:NC * t + NC], T.lt[0:1, :], F.Copy))
-        dma("y", "dlv", 16 * (t + 1), ["lvs%d" % t], [], T.lv[t:t + 1, :], T.lvs[0:1, NC * t:NC * t + NC])
-        run("v", ["lt", "dg"], ["ld"], lambda q: q.tensor_tensor(T.ld[:], T.lt[:], T.dg[:], A.mult))
-        run("v", ["ld", "m16"], ["ls"], lambda q: q.tensor_tensor_scan(T.ls[:], T.m16[:], T.ld[:], 0.0, A.mult, A.add))
-        ov = T["ov%d" % t]
-        run("v", ["ls"], ["ov%d" % t], lambda q: q.tensor_copy(ov[:], T.ls[:, 15:NC:16]))
-        ql, qls = T["ql%d" % t], T["qls%d" % t]
-        here = ["planein%d" % t, "matein%d" % t, "om"]
-        run("s", here + ["reps%d" % t], ["qls%d" % t], lambda q: q.activation(
-            qls[:], lands[:].indirect(T.om[:]), F.Copy))
-        run("v", here + ["rep%d" % t], ["ql%d" % t], lambda q: q.tensor_copy(
-            ql[:].bitcast(u32), land[:].bitcast(u32).indirect(T.om[:])))
-        bank = [("pva", T.pv[:, 0:256]), ("pvb", T.pv[:, 512:768]), ("pb", T.pb[:, 0:256]), ("ps", T.ps[:, 0:256])]
-        for b in range(4):
-            e, es = unit(0, b)
-            run("t", ["e0%d" % b, "ql%d" % t, "qls%d" % t], [bank[b][0]], lambda q: q.matmul_mx(
-                bank[b][1], e, es, ql[:], qls[:], True, True))
-        for b in range(4):
-            run("v", [bank[b][0], "m8"], ["vs%d" % b], lambda q: q.tensor_tensor_scan(
-                T.vs[:, 256 * b:256 * b + 256], T.m8[:], bank[b][1], 0.0, A.mult, A.add))
-        for b in range(4):
-            out, in_ = T.vt[:, b:4 * L:4], T.vs[:, 256 * b + 7:256 * b + 256:8]
-            if b < 3:
-                run("s", ["vs%d" % b], ["vt%d" % b], lambda q: q.activation(out, in_, F.Copy))
-            else:
-                run("v", ["vs%d" % b], ["vt%d" % b], lambda q: q.tensor_copy(out, in_))
+            run("v", ["va%d0" % b, "va%d1" % b, "m8", "m8z"], ["vs%d" % b], lambda q: q.tensor_tensor_scan(
+                T.vs[:, b:1024:4], T.m8[:], T.va[:, 256 * b:256 * b + 256], 0.0, A.mult, A.add))
         qv, qvs = T["qv%d" % t], T["qvs%d" % t]
-        run("v", ["vt0", "vt1", "vt2", "vt3", "vtp"], ["qv%d" % t], lambda q: q.quantize_mx(qv[:], qvs[:], T.vt[:]))
+        run("v", ["vs0", "vs1", "vs2", "vs3"], ["qv%d" % t], lambda q: q.quantize_mx(qv[:], qvs[:], T.vs[:]))
         vv, vvs = T["vv%d" % t], T["vvs%d" % t]
         run("s", ["qv%d" % t, "ov%d" % t], ["vvs%d" % t], lambda q: q.activation(vvs[:], qvs[:].indirect(ov[:]), F.Copy))
         run("v", ["qv%d" % t, "ov%d" % t], ["vv%d" % t], lambda q: q.tensor_copy(
@@ -306,7 +337,6 @@ def rank_program(g, core, T, topo):
             e, es = unit(2, b)
             run("t", ["e2%d" % b, "vv%d" % t, "vvs%d" % t], ["px%d" % b], lambda q: q.matmul_mx(
                 T.px[:, 512 * b:512 * b + NC], e, es, vv[:], vvs[:], False, True))
-        hn = T["h%d" % (t + 1)]
         for b in range(4):
             out, in_ = hn[:, b:4 * NC:4], T.px[:, 512 * b:512 * b + NC]
             if b % 2 == 0:
@@ -318,15 +348,15 @@ def rank_program(g, core, T, topo):
 
     qx, sx = T["qx%d" % R], T["sx%d" % R]
     kx = "qx%d" % R
-    run("t", ["qz", kx], ["pb"], lambda q: q.matmul_mx(
-        T.pb[:, 0:NC], T.qz[:], T.sz[:], qx[:, 0:NC], sx[:, 0:NC], True, True))
+    run("t", ["qz", kx], ["b0"], lambda q: q.matmul_mx(
+        bank(0, NC), T.qz[:], T.sz[:], qx[:, 0:NC], sx[:, 0:NC], True, True))
     total = 16 * 6
     dma("y", "dout", total, [kx], [], T.oc[:], qx[:, 0:NC].bitcast(u8))
     for k in range(4):
         dma("s", "dout", total, [kx], [], T.osc[4 * k:4 * k + 4, :], sx[32 * k:32 * k + 4, 0:NC])
-    run("v", ["pb"], ["ysb"], lambda q: q.tensor_copy(T.ysb[:], T.pb[:, 0:NC]))
+    run("v", ["b0"], ["ysb"], lambda q: q.tensor_copy(T.ysb[:], bank(0, NC)))
     dma("y", "dout", total, ["ysb"], [], T.y[:], T.ysb[:])
-    wait("g", ("sent", R * 2 * (len(topo.engines(core, peers[0])) + len(topo.engines(core, mate)))))
+    wait("g", ("sent", R * (2 * len(topo.engines(core, peers[0])) + 4 * len(topo.engines(core, mate)))))
     finish("g")
     wait("g", ("dlv", 16 * R))
     wait("g", ("dout", total))

from concourse.bass import DstId, RemoteDMATransfer
from concourse.mybir import dt, AluOpType, ActivationFunctionType

NC, L, R, PL = 192, 32, 3, 5
W = NC + 2
P, FLOOR, NONE, DEEP = 2.0 ** 76, -2.0 ** 74, -2.0 ** 72, -2.0 ** 80
X4, BF, F32, U8, I32, U16 = "float8_e4m3fn_x4", "bfloat16", "float32", "uint8", "int32", "uint16"

SCRATCH = {
    "wb": ("sbuf", [128, 576], BF), "zt": ("sbuf", [128, 512], BF),
    "qwb": ("sbuf", [128, 144], X4), "swb": ("sbuf", [128, 144], U8),
    "qz": ("sbuf", [128, 128], X4), "sz": ("sbuf", [128, 128], U8),
    "gone": ("sbuf", [128, 520], BF), "g1": ("sbuf", [128, 520], BF), "g8": ("sbuf", [128, 520], BF),
    "gm": ("sbuf", [128, 520], BF),
    "qe": ("sbuf", [128, 12 * 128], X4), "se": ("sbuf", [128, 12 * 128], U8),
    "u": ("sbuf", [128, 128], BF), "ut": ("sbuf", [128, 128], BF), "gk": ("sbuf", [128, 512], BF),
    "qc": ("sbuf", [128, 3 * 128], X4), "sc": ("sbuf", [128, 3 * 128], U8),
    "bq": ("sbuf", [128, 4 * W], BF), "qb": ("sbuf", [128, W], X4), "sb": ("sbuf", [128, W], U8),
    "m8": ("sbuf", [128, 256], BF), "m16": ("sbuf", [128, NC], BF),
    "idg": ("sbuf", [128, NC], I32), "idh": ("sbuf", [128, NC], I32), "dg": ("sbuf", [128, NC], BF),
    "neg": ("sbuf", [128, W], BF),
    "ip": ("sbuf", [128, 8], I32), "jb": ("sbuf", [128, 16], I32), "ja": ("sbuf", [128, 8], I32),
    "ik": ("sbuf", [128, 8], I32), "jc": ("sbuf", [128, 8], I32), "jd": ("sbuf", [128, 8], I32),
    "je": ("sbuf", [128, 8], I32), "jf": ("sbuf", [128, 8], I32), "om": ("sbuf", [128, 8], U16),
    "rm0": ("sbuf", [128, W], F32), "rm1": ("sbuf", [128, W], F32),
    "sg0": ("sbuf", [128, NC], BF), "sg1": ("sbuf", [128, NC], BF), "ix": ("sbuf", [128, 4], F32),
    "lt": ("sbuf", [128, NC], BF), "ld": ("sbuf", [128, NC], BF), "ls": ("sbuf", [128, NC], F32),
    "lvs": ("sbuf", [128, R * NC], F32),
    "va": ("sbuf", [128, 1024], BF), "vs": ("sbuf", [128, 1024], BF), "ysb": ("sbuf", [128, NC], F32),
    "pv": ("psum", [128, 2048], F32), "px": ("psum", [128, 2048], F32),
}
for _t in range(R + 1):
    SCRATCH["h%d" % _t] = ("sbuf", [128, 4 * W], BF)
    SCRATCH["qx%d" % _t] = ("sbuf", [128, W], X4)
    SCRATCH["sx%d" % _t] = ("sbuf", [128, W], U8)
for _t in range(R):
    for _n, _w in (("ws", 128), ("la", 128), ("lb", 128), ("qa", 128), ("qm", 128), ("qv", 256), ("vv", NC)):
        SCRATCH["%s%d" % (_n, _t)] = ("sbuf", [128, _w], X4)
        SCRATCH["%ss%d" % (_n, _t)] = ("sbuf", [128, _w], U8)
    SCRATCH["wl%d" % _t] = ("sbuf", [128, 8], U16)
    SCRATCH["of%d" % _t] = ("sbuf", [128, 2], U16)
    SCRATCH["ov%d" % _t] = ("sbuf", [128, 12], U16)

SEMAPHORES = ["cv", "cs", "ct", "cg", "dx", "dw", "dz", "dlv", "dout", "sent"]
SEMAPHORES += ["%s%d" % (_n, _t) for _n in ("planec", "planes", "matec", "mates") for _t in range(R)]

COUNTER = {"v": "cv", "s": "cs", "t": "ct", "g": "cg"}


def _scheduler(g, T):
    queue = {"v": g.vector, "s": g.scalar, "t": g.tensor, "g": g, "y": g.sync}
    count = {"cv": 0, "cs": 0, "ct": 0, "cg": 0}
    clock = {q: {} for q in queue}
    known = {}
    writer, readers = {}, {}

    def wait(q, token):
        name, value = token
        if clock[q].get(name, 0) >= value:
            return
        queue[q].wait_ge(T.sem[name], value)
        for n, v in list(known.get(token, {}).items()) + [token]:
            clock[q][n] = max(clock[q].get(n, 0), v)

    def need(q, reads, writes):
        tokens = {}
        own = COUNTER.get(q)
        for k in list(reads) + list(writes):
            if k in writer:
                n, v = writer[k]
                tokens[n] = max(tokens.get(n, 0), v)
        for k in writes:
            for n, v in readers.get(k, []):
                if n != own:
                    tokens[n] = max(tokens.get(n, 0), v)
        for n in sorted(tokens):
            wait(q, (n, tokens[n]))

    def note(q, token, reads, writes):
        known[token] = dict(clock[q])
        for k in reads:
            readers.setdefault(k, []).append(token)
        for k in writes:
            writer[k] = token
            readers[k] = []

    def run(q, reads, writes, call):
        need(q, reads, writes)
        name = COUNTER[q]
        call(queue[q]).then_inc(T.sem[name], 1)
        count[name] += 1
        note(q, (name, count[name]), reads, writes)

    def dma(q, sem, value, reads, writes, out, in_):
        need(q, reads, writes)
        queue[q].dma_start(out, in_).then_inc(T.sem[sem], 16)
        note(q, (sem, value), reads, writes)

    def arrive(token, writes):
        for k in writes:
            writer[k] = token
            readers[k] = []

    def finish(q):
        for name in sorted(count):
            if count[name]:
                wait(q, (name, count[name]))

    return run, dma, need, wait, arrive, finish


def rank_program(g, core, T, topo):
    rank = T.rank_of(core)
    if rank is None:
        return
    A, F = AluOpType, ActivationFunctionType
    run, dma, need, wait, arrive, finish = _scheduler(g, T)
    u8, u32 = dt.uint8, dt.uint32

    cores = list(T.cores)
    first = [c for c in cores if c == cores[0] or topo.same_plane(c, cores[0])]
    planes = [first, [c for c in cores if c not in first]]
    mine = 0 if core in first else 1
    me = planes[mine].index(core)
    mate = planes[1 - mine][me]
    assert topo.mates(core, mate)
    for a in range(2):
        for i in range(4):
            assert planes[a][i] == cores[2 * i + a]
    peers = [c for c in planes[mine] if c != core]

    def bank(b, n):
        return T.pv[:, 512 * b:512 * b + n]

    dma("s", "dw", 16, [], ["wb"], T.wb[:, 0:128], T.w[:, 0:128])
    dma("y", "dx", 16, [], ["h0"], T.h0[:, 0:4 * NC], T.x[:])
    dma("y", "dz", 16, [], ["zt"], T.zt[:], T.z[:])
    run("g", [], ["ip"], lambda q: q.iota(T.ip[:], [[0, 8]], 0, 1))
    run("g", [], ["bqc"], lambda q: q.iota(T.bq[:], [[0, 4 * W]], 1, 0, allow_small_or_imprecise_dtypes=True))
    run("g", ["bqc"], ["bqp"], lambda q: q.iota(
        T.bq[:, 4 * NC:4 * W], [[0, 4 * W - 4 * NC]], 2, 0, allow_small_or_imprecise_dtypes=True))
    run("v", [], ["wbz"], lambda q: q.memset(T.wb[:, 128:576], 0.0))
    run("v", [], ["wl0"], lambda q: q.memset(T.wl0[:], 6))
    run("v", [], ["hp0"], lambda q: q.memset(T.h0[:, 4 * NC:4 * W], 0.0))
    run("v", [], ["gone"], lambda q: q.memset(T.gone[:], 1.0))
    run("g", ["gone"], ["g1"], lambda q: q.affine_select(T.g1[:], T.gone[:], [[-1, 520]], A.is_equal, 0.0, 4, 4))
    run("g", [], ["ja"], lambda q: q.iota(T.ja[:], [[4, 8]], 0, 0))
    run("g", [], ["ik"], lambda q: q.iota(T.ik[:], [[0, 8]], L * (4 - me), L))
    run("g", [], ["idg"], lambda q: q.iota(T.idg[:], [[1, NC]], 128, -1))

    def laid(k):
        run("v", ["u", "u0", "u1", "u2", "u3", "u4"], ["ut"], lambda q: q.transpose(T.ut[:], T.u[:]))
        run("v", ["ut", "gkz"], ["gk0"], lambda q: q.tensor_copy(T.gk[:, 0:512:4], T.ut[:]))
        run("v", ["gk0", "gk1", "gkz"], ["qc%d" % k], lambda q: q.quantize_mx(
            T.qc[:, 128 * k:128 * k + 128], T.sc[:, 128 * k:128 * k + 128], T.gk[:]))

    def const(k):
        return T.qc[:, 128 * k:128 * k + 128], T.sc[:, 128 * k:128 * k + 128]

    run("v", [], ["u"], lambda q: q.memset(T.u[:], 0.0))
    run("v", [], ["gkz"], lambda q: q.memset(T.gk[:], 0.0))
    for i in range(PL - 1):
        run("v", ["ip"], ["jb%d" % i], lambda q: q.tensor_scalar(
            T.jb[0:32, 4 * i:4 * i + 4], T.ip[0:32, 0:4], 1 << i, None, A.bitwise_and))
    for i in range(PL - 1):
        run("v", ["jb%d" % i, "u"], ["u%d" % i], lambda q: q.tensor_scalar(
            T.u[0:32, i:128:32], T.jb[0:32, 4 * i:4 * i + 4], 2 * P / (1 << i), P, A.mult, A.subtract))
    run("v", ["u"], ["u4"], lambda q: q.memset(T.u[0:32, 4:128:32], -P))
    run("v", ["gkz"], ["gk1"], lambda q: q.memset(T.gk[:, 1:512:4], -P * PL / 2 / 128))
    laid(0)
    run("v", ["u"], ["u4"], lambda q: q.memset(T.u[0:32, 4:128:32], P))
    laid(1)
    run("v", [], ["neg"], lambda q: q.memset(T.neg[:], DEEP))
    run("v", ["neg"], ["negp"], lambda q: q.memset(T.neg[:, NC:W], NONE))
    run("v", ["wb", "wbz"], ["qwb"], lambda q: q.quantize_mx(T.qwb[:], T.swb[:], T.wb[:]))

    def strength_tile(t):
        ws, wss, wl = T["ws%d" % t], T["wss%d" % t], T["wl%d" % t]
        run("s", ["qwb", "wl%d" % t], ["wss%d" % t], lambda q: q.activation(
            wss[:], T.swb[:].indirect(wl[:]), F.Copy))
        run("v", ["qwb", "wl%d" % t], ["ws%d" % t], lambda q: q.tensor_copy(
            ws[:].bitcast(u32), T.qwb[:].bitcast(u32).indirect(wl[:])))

    strength_tile(0)
    run("v", ["h0", "hp0"], ["qx0"], lambda q: q.quantize_mx(T.qx0[:], T.sx0[:], T.h0[:]))

    def unit_tiles(s, name):
        src = T[name]
        for b in range(4):
            o = 128 * (4 * s + b)
            run("v", [name], ["e%d%d" % (s, b)], lambda q: q.quantize_mx(
                T.qe[:, o:o + 128], T.se[:, o:o + 128], src[:, 4 - b:516 - b]))

    def unit(s, b):
        o = 128 * (4 * s + b)
        return T.qe[:, o:o + 128], T.se[:, o:o + 128]

    def first_constants():
        unit_tiles(1, "g1")
        run("s", ["g1"], ["g8"], lambda q: q.activation(T.g8[:], T.g1[:], F.Copy, scale=0.125))
        run("s", ["g1"], ["gm"], lambda q: q.activation(T.gm[:], T.g1[:], F.Copy, scale=-0.5))
        run("v", [], ["u"], lambda q: q.memset(T.u[:], 0.0))
        for i in range(PL):
            run("v", ["u"], ["u%d" % i], lambda q: q.memset(T.u[0:32, i:128:32], 2.0 ** i))
        run("v", ["gkz"], ["gk1"], lambda q: q.memset(T.gk[:, 1:512:4], 0.0))
        laid(2)
        run("v", ["idg"], ["idh"], lambda q: q.tensor_scalar(T.idh[:], T.idg[:], 15, None, A.bitwise_and))
        run("v", [], ["m16"], lambda q: q.memset(T.m16[:], 1.0))
        run("v", ["idh"], ["dg"], lambda q: q.tensor_scalar(T.dg[:], T.idh[:], 0.0, None, A.is_equal))
        run("v", ["m16"], ["m16z"], lambda q: q.memset(T.m16[:, 0:NC:16], 0.0))
        run("v", ["ip"], ["jc"], lambda q: q.tensor_scalar(
            T.jc[:], T.ip[:], 2, 3, A.arith_shift_right, A.bitwise_and))
        run("v", ["ik"], ["jd"], lambda q: q.tensor_scalar(T.jd[:], T.ik[:], 3 * L, None, A.bitwise_and))
        run("v", ["jc", "ja"], ["je"], lambda q: q.tensor_tensor(T.je[:], T.ja[:], T.jc[:], A.add))
        run("v", [], ["m8"], lambda q: q.memset(T.m8[:], 1.0))
        run("v", ["jd", "je"], ["jf"], lambda q: q.tensor_tensor(T.jf[:], T.je[:], T.jd[:], A.add))
        run("v", ["m8"], ["m8z"], lambda q: q.memset(T.m8[:, 0:256:8], 0.0))
        run("v", ["jf"], ["om"], lambda q: q.tensor_copy(T.om[:], T.jf[:]))

    half = (2 ** PL - 1) / 2
    for t in range(R):
        qx, sx = T["qx%d" % t], T["sx%d" % t]
        kx = "qx%d" % t
        la, las, lb, lbs = T["la%d" % t], T["las%d" % t], T["lb%d" % t], T["lbs%d" % t]
        run("t", ["qwb", kx], ["b0"], lambda q: q.matmul_mx(
            bank(0, W), T.qwb[:, 8 * t:8 * t + 128], T.swb[:, 8 * t:8 * t + 128], qx[:], sx[:], True, True))
        for c in range(2):
            run("t", ["ws%d" % t, "wss%d" % t, kx], ["b%d" % (1 + c)], lambda q: q.matmul_mx(
                bank(1 + c, W), T["ws%d" % t][:], T["wss%d" % t][:], qx[:], sx[:], True, False))
        run("v", ["b0", "bqc", "bqp"], ["bq"], lambda q: q.tensor_scalar(
            T.bq[:, 0:4 * W:4], bank(0, W), 0.0, 0.5, A.is_lt, A.subtract))
        run("v", ["bq"], ["qb"], lambda q: q.quantize_mx(T.qb[:], T.sb[:], T.bq[:]))
        for c in range(2):
            e, es = const(c)
            run("t", ["qc%d" % c, "qb"], ["b%d" % (1 + c)], lambda q: q.matmul_mx(
                bank(1 + c, W), e, es, T.qb[:], T.sb[:], False, True))
        for c in range(2):
            rm, sg = T["rm%d" % c], T["sg%d" % c]
            run("v", ["b%d" % (1 + c), "neg", "negp"], ["rm%d" % c], lambda q: q.tensor_tensor_scan(
                rm[:], bank(1 + c, W), T.neg[:], FLOOR, A.max, A.max))
            run("s", ["rm%d" % c], ["sg%d" % c, "ix%d" % c], lambda q: q.activation(
                sg[:], rm[:, 0:NC], F.Sign, bias=rm[:, NC:NC + 1], scale=-1.0, accum_out=T.ix[:, c:c + 1]))
        of = T["of%d" % t]
        run("v", ["ix0", "ix1"], ["of%d" % t], lambda q: q.tensor_copy(of[:], T.ix[:, 0:2]))
        run("s", [kx, "of%d" % t], ["reps%d" % t], lambda q: q.activation(
            las[:, 0:L], sx[:].indirect(of[:]), F.Copy))
        run("v", [kx, "of%d" % t], ["rep%d" % t], lambda q: q.tensor_copy(
            la[:, 0:L].bitcast(u32), qx[:].bitcast(u32).indirect(of[:])))
        ids, slot = [], []
        for c in peers:
            rid, pid = topo.addr(c, core)
            ids.append(DstId(rid=rid, pnc=pid))
            slot.append(L * ((me - planes[mine].index(c)) % 4))
        mask = topo.mask(core, peers[0])
        need("g", ["rep%d" % t], [])
        g.remote_dma_fused([RemoteDMATransfer(
            dst_ids=ids, dma_engine_mask=mask, remote_sem=T.sem["planec%d" % t], srcs=[la[:, 0:L].bitcast(u8)],
            dsts=[la[:, o:o + L].bitcast(u8) for o in slot])], local_sem=T.sem.sent)
        need("g", ["reps%d" % t], [])
        g.remote_dma_fused([RemoteDMATransfer(
            dst_ids=ids, dma_engine_mask=mask, remote_sem=T.sem["planes%d" % t], srcs=[las[:, 0:L]],
            dsts=[las[:, o:o + L] for o in slot])], local_sem=T.sem.sent)
        n = len(topo.engines(core, peers[0])) * len(peers)
        arrive(("planec%d" % t, n), ["pc%d" % t])
        arrive(("planes%d" % t, n), ["ps%d" % t])
        rid, pid = topo.addr(mate, core)
        mask = topo.mask(core, mate)
        mc, ms = T.sem["matec%d" % t], T.sem["mates%d" % t]
        g.remote_dma(lb[:, 0:L].bitcast(u8), la[:, 0:L].bitcast(u8), mc, T.sem.sent, pid, rid, mask)
        g.remote_dma(lbs[:, 0:L], las[:, 0:L], ms, T.sem.sent, pid, rid, mask)
        need("g", ["pc%d" % t], [])
        g.remote_dma(lb[:, L:4 * L].bitcast(u8), la[:, L:4 * L].bitcast(u8), mc, T.sem.sent, pid, rid, mask)
        need("g", ["ps%d" % t], [])
        g.remote_dma(lbs[:, L:4 * L], las[:, L:4 * L], ms, T.sem.sent, pid, rid, mask)
        n = 2 * len(topo.engines(core, mate))
        arrive(("matec%d" % t, n), ["mc%d" % t])
        arrive(("mates%d" % t, n), ["ms%d" % t])
        if t == 0:
            first_constants()
        e, es = const(2)
        run("t", ["qc2", "qb"], ["b3"], lambda q: q.matmul_mx(
            bank(3, NC), e, es, T.qb[:, 0:NC], T.sb[:, 0:NC], True, True))
        for b in range(4):
            e, es = unit(1, b)
            run("t", ["e1%d" % b, kx], ["px%d" % b], lambda q: q.matmul_mx(
                T.px[:, 512 * b:512 * b + NC], e, es, qx[:, 0:NC], sx[:, 0:NC], True, False))
        run("s", ["b3"], ["lt"], lambda q: q.activation(T.lt[:], bank(3, NC), F.Copy))
        run("s", ["b3"], ["lvs%d" % t], lambda q: q.activation(
            T.lvs[0:1, NC * t:NC * t + NC], T.pv[0:1, 3 * 512:3 * 512 + NC], F.Identity, bias=half))
        dma("y", "dlv", 16 * (t + 1), ["lvs%d" % t], [], T.lv[t:t + 1, :], T.lvs[0:1, NC * t:NC * t + NC])
        run("v", ["lt", "dg"], ["ld"], lambda q: q.tensor_tensor(T.ld[:], T.lt[:], T.dg[:], A.mult))
        run("v", ["ld", "m16", "m16z"], ["ls"], lambda q: q.tensor_tensor_scan(
            T.ls[:], T.m16[:], T.ld[:], 0.0, A.mult, A.add))
        ov = T["ov%d" % t]
        run("v", ["ls"], ["ov%d" % t], lambda q: q.tensor_scalar(
            ov[:], T.ls[:, 15:NC:16], 8.0, 8.0 * half + 7.0, A.mult, A.add))
        if t == 0:
            unit_tiles(0, "g8")

        def plane_values(src, srcs, out, outs, kq, kc, ks, a, engine):
            run("v", kc + ["om"], [kq], lambda q: q.tensor_copy(
                out[:].bitcast(u32), src[:].bitcast(u32).indirect(T.om[:])))
            run("s", ks + ["om"], [kq + "s"], lambda q: q.activation(outs[:], srcs[:].indirect(T.om[:]), F.Copy))
            for b in range(4):
                e, es = unit(0, b)
                run("t", ["e0%d" % b, kq, kq + "s"], ["b%d" % b], lambda q: q.matmul_mx(
                    bank(b, 4 * L), e, es, out[:], outs[:], True, True))
            for b in range(4):
                place = T.va[:, 256 * b + a:256 * b + 256:2]
                if engine[b] == "s":
                    run("s", ["b%d" % b], ["va%d%d" % (b, a)], lambda q: q.activation(place, bank(b, 4 * L), F.Copy))
                else:
                    run("v", ["b%d" % b], ["va%d%d" % (b, a)], lambda q: q.tensor_copy(place, bank(b, 4 * L)))

        plane_values(la, las, T["qa%d" % t], T["qas%d" % t], "qa%d" % t, ["rep%d" % t, "pc%d" % t],
                     ["reps%d" % t, "ps%d" % t], mine, "ssss")
        if t == 0:
            unit_tiles(2, "gm")
        if t == 1:
            run("v", ["zt"], ["qz"], lambda q: q.quantize_mx(T.qz[:], T.sz[:], T.zt[:]))
        if t + 1 < R:
            run("v", [], ["wl%d" % (t + 1)], lambda q: q.memset(T["wl%d" % (t + 1)][:], 8 * (t + 1) + 6))
            strength_tile(t + 1)
        hn = T["h%d" % (t + 1)]
        run("v", [], ["hp%d" % (t + 1)], lambda q: q.memset(hn[:, 4 * NC:4 * W], 0.0))
        plane_values(lb, lbs, T["qm%d" % t], T["qms%d" % t], "qm%d" % t, ["mc%d" % t], ["ms%d" % t], 1 - mine, "vsss")
        for b in range(4):
            run("v", ["va%d0" % b, "va%d1" % b, "m8", "m8z"], ["vs%d" % b], lambda q: q.tensor_tensor_scan(
                T.vs[:, b:1024:4], T.m8[:], T.va[:, 256 * b:256 * b + 256], 0.0, A.mult, A.add))
        qv, qvs = T["qv%d" % t], T["qvs%d" % t]
        run("v", ["vs0", "vs1", "vs2", "vs3"], ["qv%d" % t], lambda q: q.quantize_mx(qv[:], qvs[:], T.vs[:]))
        vv, vvs = T["vv%d" % t], T["vvs%d" % t]
        run("s", ["qv%d" % t, "ov%d" % t], ["vvs%d" % t], lambda q: q.activation(vvs[:], qvs[:].indirect(ov[:]), F.Copy))
        run("v", ["qv%d" % t, "ov%d" % t], ["vv%d" % t], lambda q: q.tensor_copy(
            vv[:].bitcast(u32), qv[:].bitcast(u32).indirect(ov[:])))
        for b in range(4):
            e, es = unit(2, b)
            run("t", ["e2%d" % b, "vv%d" % t, "vvs%d" % t], ["px%d" % b], lambda q: q.matmul_mx(
                T.px[:, 512 * b:512 * b + NC], e, es, vv[:], vvs[:], False, True))
        for b in range(4):
            out, in_ = hn[:, b:4 * NC:4], T.px[:, 512 * b:512 * b + NC]
            if b % 2 == 0:
                run("s", ["px%d" % b], ["h%d%d" % (t + 1, b)], lambda q: q.activation(out, in_, F.Copy))
            else:
                run("v", ["px%d" % b], ["h%d%d" % (t + 1, b)], lambda q: q.tensor_copy(out, in_))
        run("v", ["h%d%d" % (t + 1, b) for b in range(4)] + ["hp%d" % (t + 1)], ["qx%d" % (t + 1)],
            lambda q: q.quantize_mx(T["qx%d" % (t + 1)][:], T["sx%d" % (t + 1)][:], hn[:]))

    qx, sx = T["qx%d" % R], T["sx%d" % R]
    kx = "qx%d" % R
    run("t", ["qz", kx], ["b0"], lambda q: q.matmul_mx(
        bank(0, NC), T.qz[:], T.sz[:], qx[:, 0:NC], sx[:, 0:NC], True, True))
    total = 16 * 6
    dma("y", "dout", total, [kx], [], T.oc[:], qx[:, 0:NC].bitcast(u8))
    for k in range(4):
        dma("s", "dout", total, [kx], [], T.osc[4 * k:4 * k + 4, :], sx[32 * k:32 * k + 4, 0:NC])
    run("v", ["b0"], ["ysb"], lambda q: q.tensor_copy(T.ysb[:], bank(0, NC)))
    dma("y", "dout", total, ["ysb"], [], T.y[:], T.ysb[:])
    wait("g", ("sent", R * (2 * len(topo.engines(core, peers[0])) + 4 * len(topo.engines(core, mate)))))
    finish("g")
    wait("g", ("dlv", 16 * R))
    wait("g", ("dout", total))
